import numpy as np
import ml_dtypes


def mxq(x, axis, fmt="e4m3"):
    dtype, down = {"e4m3": (ml_dtypes.float8_e4m3fn, 7), "e5m2": (ml_dtypes.float8_e5m2, 14)}[fmt]
    v = np.moveaxis(np.asarray(x, np.float32).astype(ml_dtypes.bfloat16).astype(np.float64), axis, -1)
    blocks = v.reshape(v.shape[:-1] + (-1, 32))
    amax = np.abs(blocks).max(-1, keepdims=True)
    byte = np.maximum(np.where(amax > 0, np.frexp(amax)[1] - 1 + 127, 0) - down, 1)
    scale = np.exp2(byte - 127.0)
    codes = (blocks / scale).astype(np.float32).astype(dtype).astype(np.float64)
    return np.moveaxis((codes * scale).reshape(v.shape), -1, axis)


WIDE = False


def mx_kscale(k):
    if not WIDE:
        return np.ones(k)
    levels = np.array([10, -10, 5, -5, 0])
    if k % 512:
        return np.exp2(np.random.permutation(np.resize(levels, k // 32))).repeat(32)
    a = np.empty((k // 512, 16))
    for p in range(k // 512):
        a[p, :8] = np.random.permutation(np.resize(levels, 8))
        for g in range(8):
            far = levels[np.abs(levels - a[p, g]) >= 10]
            a[p, g + 8] = far[np.random.randint(len(far))]
    return np.exp2(a.ravel()).repeat(32)


def f64(x):
    return np.asarray(x).astype(np.float64)


def striped(idx):
    return np.tile(idx.reshape(-1, 16).T, (8, 1)).astype(np.uint16)


def unstriped(offs):
    return offs[:16].T.reshape(-1).astype(np.int64)


def striped8(idx):
    return np.concatenate([x.reshape(-1, 16).T for x in idx]).astype(np.uint16)


def runs(offs, k):
    lists = np.stack([offs[16 * r : 16 * r + 16].T.reshape(-1) for r in range(8)]).astype(np.int64)
    return lists[np.arange(k) % 512 // 64]


def pack_weight(w):
    k, n = w.shape
    w = f64(np.asarray(w, np.float32).astype(ml_dtypes.bfloat16)).reshape(k // 32, 32, n)
    amax = np.abs(w).max(1)
    byte = np.clip(np.where(amax > 0, np.frexp(amax)[1] - 1 + 127 - 7, 1), 1, 254)
    scaled = (w * np.exp2(127.0 - byte)[:, None, :]).reshape(k, n).astype(np.float32)
    words = np.ascontiguousarray(scaled.reshape(k // 512, 128, 4, n).transpose(0, 1, 3, 2)).astype(ml_dtypes.float8_e4m3fn).view(np.uint8)
    return words, np.ascontiguousarray(byte.astype(np.uint8).reshape(k // 512, 16, n))


def unpack_weight(words, scales):
    g, p, n, _ = words.shape
    vals = np.ascontiguousarray(words).view(ml_dtypes.float8_e4m3fn).astype(np.float64) * np.repeat(np.exp2(scales.astype(np.float64) - 127.0), 8, axis=1)[..., None]
    return vals.transpose(0, 1, 3, 2).reshape(g * 512, n)

def planes(y):
    n, m = y.shape
    v = y.astype(np.float32).astype(ml_dtypes.bfloat16).astype(np.float64).reshape(n // 32, 32, m)
    top = np.abs(v).max(1)
    byte = np.clip(np.where(top > 0, np.frexp(top)[1] - 1 + 127 - 7, 1), 1, 254)
    codes = (v * np.exp2(127.0 - byte)[:, None, :]).reshape(n, m).astype(np.float32).astype(ml_dtypes.float8_e4m3fn).view(np.uint8)
    words = codes.reshape(n // 512, 128, 4, m).transpose(0, 1, 3, 2)
    return np.ascontiguousarray(words), np.ascontiguousarray(byte.astype(np.uint8).reshape(n // 512, 16, m))


K, T, S, N, H = 512, 2048, 512, 512, 512


def setup_inputs():
    n = np.random.standard_normal
    s = mx_kscale(K)[:, None]
    u = mx_kscale(S)
    packed_xT = pack_weight(n((K, T)) * s)
    packed_w1 = pack_weight(n((S, N)) / np.sqrt(S) / u[:, None])
    return {
        "x_words": packed_xT[0],
        "x_scales": packed_xT[1],
        "wa": (n((K, H)) / np.sqrt(K) / s).astype(np.float32),
        "wb": (n((K, H)) / np.sqrt(K) / s).astype(np.float32),
        "gt": (np.random.uniform(0.5, 1.5, (S, 1)) * u[:, None]).astype(np.float32),
        "w1_words": packed_w1[0],
        "w1_scales": packed_w1[1],
        "offs": striped(np.random.permutation(T)[:S]),
        "two": striped(np.random.permutation(T)[:S]),
        "n1": striped8(np.stack([np.random.permutation(H) for _ in range(8)])),
        "n2": striped8(np.stack([np.random.permutation(H) for _ in range(8)])),
        "n3": striped8(np.stack([np.random.permutation(H) for _ in range(8)])),
        "n4": striped8(np.stack([np.random.permutation(H) for _ in range(8)])),
    }


def reference(x_words, x_scales, wa, wb, gt, w1_words, w1_scales, offs, two, n1, n2, n3, n4):
    xq = unpack_weight(x_words, x_scales)[:, unstriped(offs)]
    y = xq.T @ mxq(f64(wa), 0, "e4m3")
    x_two = unpack_weight(x_words, x_scales)[:, unstriped(two)]
    d = x_two.T @ mxq(f64(wb), 0, "e4m3")
    z = f64(gt) * (0.75 * (y * (d[np.arange(S)[:, None], runs(n2, S)]) - ((y[np.arange(S)[:, None], runs(n1, S)]) * d)))
    h = unpack_weight(w1_words, w1_scales).T @ mxq(z, 0, "e4m3")
    pa = h[np.arange(N)[:, None], runs(n3, N)]
    pb = h[np.arange(N)[:, None], runs(n4, N)]
    mu = 0.3125 * (h + pa + pb)
    out_0 = (h - mu) / (np.sqrt((pa - mu) ** 2 + (pb - mu) ** 2 + 0.25))
    return (out_0,) + planes(out_0)

@@ -1,0 +1,246 @@
+from contextlib import ExitStack
+
+import concourse.mybir as mybir
+from concourse.masks import make_identity
+
+K, T, S, N, H = 512, 2048, 512, 512, 512
+FLOPS = 2 * 3 * 512 * 512 * 512
+F32 = mybir.dt.float32
+BF16 = mybir.dt.bfloat16
+I32 = mybir.dt.int32
+U32 = mybir.dt.uint32
+U16 = mybir.dt.uint16
+U8 = mybir.dt.uint8
+FP8X4 = mybir.dt.float8_e4m3fn_x4
+ALU = mybir.AluOpType
+ACT = mybir.ActivationFunctionType
+P = 128
+G_CHUNKS = ((0, 256), (256, 128), (384, 128))
+OUT_W = 128
+G_BUFS = 4
+
+
+def tile_picked_twtcrossbstd_none_po_kernel(
+    tc, x_words, x_scales, wa, wb, gt, w1_words, w1_scales, offs, two, n1, n2, n3, n4, out_0, out_1, out_2
+):
+    nc = tc.nc
+    with ExitStack() as ctx:
+        keep = ctx.enter_context(tc.tile_pool(name="keep", bufs=1))
+        ring = ctx.enter_context(tc.tile_pool(name="ring", bufs=G_BUFS))
+        psum = ctx.enter_context(tc.psum_pool(name="psum", bufs=1))
+
+        def sb(name, shape, dtype):
+            return keep.tile(shape, dtype, name=name, align_bytes=64)
+
+        def bank(b):
+            return psum.tile([P, 512], F32, name="bank%d" % b, tag="bank%d" % b)
+
+        def load_list(name, src):
+            tile = keep.tile([P, 32], U16, name=name)
+            nc.sync.dma_start(tile[:], src)
+            return tile
+
+        def load_scale_rows(tile, src):
+            for q in range(4):
+                nc.sync.dma_start(tile[32 * q : 32 * q + 4, :].bitcast(I32), src[0, 4 * q : 4 * q + 4, :].bitcast(I32))
+
+        def deal_words(dst, src):
+            nc.vector.tensor_copy(
+                dst.bitcast(I32).rearrange("p (t c i) -> p c t i", t=4, i=4),
+                src.bitcast(I32).rearrange("p (c i t) -> p c t i", t=4, i=4),
+            )
+
+        def deal_scales(dst, src):
+            nc.vector.tensor_copy(
+                dst.rearrange("p (t c i) -> p c t i", t=4, i=16),
+                src.rearrange("p (c i t) -> p c t i", t=4, i=16),
+            )
+
+        xs = sb("xs", [P, T], U8)
+        nc.gpsimd.memset(xs[:].bitcast(I32), 0)
+        quarter = sb("quarter", [P, 1], F32)
+        nc.gpsimd.memset(quarter[:], 0.25)
+        warm = sb("warm", [P, 1], F32)
+        nc.scalar.activation(warm[:], quarter[:], ACT.Abs_reciprocal_sqrt, bias=quarter[:], scale=0.5)
+        w1s_raw = sb("w1s_raw", [P, N], U8)
+        nc.vector.memset(w1s_raw[:].bitcast(I32), 0)
+        ident = sb("ident", [P, P], F32)
+        make_identity(nc, ident[:])
+
+        w_raw = {}
+
+        def load_weight_half(name, src, half):
+            raw = sb("w%s_raw%d" % (name, half), [P, 4, 256], F32)
+            nc.sync.dma_start(raw[:], src.rearrange("(p j) c -> p j c", j=4)[:, :, 256 * half : 256 * half + 256])
+            w_raw[name, half] = raw
+
+        offs_t = load_list("offs_t", offs)
+        load_weight_half("a", wa, 0)
+        load_scale_rows(xs, x_scales)
+        two_t = load_list("two_t", two)
+        xw = sb("xw", [P, T], U32)
+        nc.sync.dma_start(xw[:].bitcast(I32), x_words[0].rearrange("p n t -> p (n t)").bitcast(I32))
+        load_weight_half("a", wa, 1)
+        load_weight_half("b", wb, 0)
+        load_weight_half("b", wb, 1)
+        gt_t = sb("gt_t", [P, 4], F32)
+        nc.sync.dma_start(gt_t[:], gt.rearrange("(p t) o -> p (t o)", t=4))
+        n1_t = load_list("n1_t", n1)
+        n2_t = load_list("n2_t", n2)
+        w1w_raw = sb("w1w_raw", [P, N], U32)
+        nc.sync.dma_start(w1w_raw[:].bitcast(I32), w1_words[0].rearrange("p n t -> p (n t)").bitcast(I32))
+        load_scale_rows(w1s_raw, w1_scales)
+        n3_t = load_list("n3_t", n3)
+        n4_t = load_list("n4_t", n4)
+
+        picked_w, picked_s = {}, {}
+        for name, lst in (("a", offs_t), ("b", two_t)):
+            g = sb("gs_" + name, [P, S], U8)
+            nc.vector.tensor_copy(g[:], xs[:].indirect(lst[:]))
+            picked_s[name] = sb("ds_" + name, [P, S], U8)
+            deal_scales(picked_s[name][:], g[:])
+
+        def pick_words(name, lst, tag):
+            g = keep.tile([P, S], U32, name="gw_" + name, tag=tag, align_bytes=64)
+            nc.vector.tensor_copy(g[:], xw[:].indirect(lst[:]))
+            picked_w[name] = sb("dw_" + name, [P, S], U32)
+            deal_words(picked_w[name][:], g[:])
+
+        w_codes = {name: sb("wc_" + name, [P, H], U32) for name in "ab"}
+        w_scales = {name: sb("ws_" + name, [P, H], U8) for name in "ab"}
+
+        def quantise_weight_half(name, half, on_vector):
+            grouped = keep.tile([P, 256, 4], BF16, name="w_bf", tag="w%s_bf%d" % (name, half), align_bytes=64)
+            dst = grouped[:].rearrange("p (c i) j -> p c j i", i=4)
+            src = w_raw[name, half][:].rearrange("p j (c i) -> p c j i", i=4)
+            if on_vector:
+                nc.vector.tensor_copy(dst, src)
+            else:
+                nc.scalar.copy(dst, src)
+            cols = slice(256 * half, 256 * half + 256)
+            nc.vector.quantize_mx(
+                out=w_codes[name][:, cols].bitcast(FP8X4), scales=w_scales[name][:, cols],
+                in_=grouped[:].rearrange("p c j -> p (c j)"))
+
+        def first_product(dst, name, t, cols):
+            rows = slice(P * t, P * t + P)
+            nc.tensor.matmul_mx(
+                out=dst, lhsT=picked_w[name][:, rows].bitcast(FP8X4), lhsT_scale=picked_s[name][:, rows],
+                rhs=w_codes[name][:, cols].bitcast(FP8X4), rhs_scale=w_scales[name][:, cols], start=True, stop=True)
+
+        quantise_weight_half("a", 0, False)
+        pick_words("a", offs_t, "gw_a")
+        quantise_weight_half("a", 1, False)
+        pick_words("b", two_t, "wa_bf1")
+        quantise_weight_half("b", 0, False)
+        y = [sb("y%d" % t, [P, H], F32) for t in range(4)]
+        d = [sb("d%d" % t, [P, H], F32) for t in range(4)]
+        for t in range(4):
+            acc = bank(t)
+            first_product(acc[:], "a", t, slice(0, H))
+            nc.scalar.activation(y[t][:], acc[:], ACT.Copy, scale=gt_t[:, t : t + 1])
+        quantise_weight_half("b", 1, True)
+        for half in range(2):
+            cols = slice(256 * half, 256 * half + 256)
+            for pair in range(2):
+                acc = bank(4 + 2 * half + pair)
+                for u in range(2):
+                    first_product(acc[:, 256 * u : 256 * u + 256], "b", 2 * pair + u, cols)
+                for u in range(2):
+                    nc.scalar.activation(d[2 * pair + u][:, cols], acc[:, 256 * u : 256 * u + 256], ACT.Copy, scale=0.75)
+
+        w1w = sb("w1w", [P, N], U32)
+        deal_words(w1w[:], w1w_raw[:])
+        w1s = sb("w1s", [P, N], U8)
+        deal_scales(w1s[:], w1s_raw[:])
+
+        h_pos = [sb("hp%d" % t, [P, H], F32) for t in range(4)]
+        h_neg = [sb("hn%d" % t, [P, H], F32) for t in range(4)]
+        xn = [sb("xn%d" % c, [P, 4, 256], F32) for c in range(2)]
+        yp = [sb("yp%d" % c, [P, 4, 256], F32) for c in range(2)]
+        for half in range(2):
+            w = 256
+            c0 = w * half
+            cols = slice(c0, c0 + w)
+            lcols = slice(c0 // 16, (c0 + w) // 16)
+            g1 = sb("zg1_%d" % c0, [P, 4, w], F32)
+            g2 = sb("zg2_%d" % c0, [P, 4, w], F32)
+            for t in range(4):
+                nc.vector.tensor_tensor(g2[:, t, :], y[t][:].indirect(n1_t[:, lcols]), d[t][:, cols], ALU.mult)
+            for t in range(4):
+                nc.vector.tensor_tensor(g1[:, t, :], d[t][:].indirect(n2_t[:, lcols]), y[t][:, cols], ALU.mult)
+            zb = sb("zb%d" % c0, [P, w, 4], BF16)
+            nc.vector.tensor_tensor(
+                zb[:].rearrange("p (c i) t -> p c t i", i=2),
+                g1[:].rearrange("p t (c i) -> p c t i", i=2),
+                g2[:].rearrange("p t (c i) -> p c t i", i=2), ALU.subtract)
+            zc = sb("zc%d" % c0, [P, w], U32)
+            zs = sb("zs%d" % c0, [P, w], U8)
+            nc.vector.quantize_mx(out=zc[:].bitcast(FP8X4), scales=zs[:], in_=zb[:].rearrange("p c t -> p (c t)"))
+            accs = [bank(2 * half + pair) for pair in range(2)]
+            parts = [accs[t // 2][:, w * (t % 2) : w * (t % 2) + w] for t in range(4)]
+            for t in range(4):
+                rows = slice(P * t, P * t + P)
+                nc.tensor.matmul_mx(
+                    out=parts[t], lhsT=w1w[:, rows].bitcast(FP8X4), lhsT_scale=w1s[:, rows],
+                    rhs=zc[:].bitcast(FP8X4), rhs_scale=zs[:], start=True, stop=True)
+            for t in range(4):
+                nc.scalar.activation(h_neg[t][:, cols], parts[t], ACT.Copy, scale=-1.0)
+            for t in range(4):
+                nc.scalar.copy(h_pos[t][:, cols], parts[t])
+            for pair in range(2):
+                nc.scalar.activation(xn[half][:, 2 * pair : 2 * pair + 2, :].rearrange("p t j -> p (t j)"), accs[pair][:],
+                                     ACT.Copy, scale=-11.0 / 5.0)
+            for pair in range(2):
+                nc.scalar.activation(yp[half][:, 2 * pair : 2 * pair + 2, :].rearrange("p t j -> p (t j)"), accs[pair][:],
+                                     ACT.Copy, scale=8.0 / 15.0)
+
+        def add_transposed(dst, terms):
+            for t in range(4):
+                for n, term in enumerate(terms):
+                    nc.tensor.matmul(dst[:, P * t : P * t + P], lhsT=term[:, t, :], rhs=ident[:],
+                                     start=(n == 0), stop=(n == len(terms) - 1), is_transpose=True)
+
+        out_codes = sb("out_codes", [P, H], U32)
+        out_scales = sb("out_scales", [P, H], U8)
+        out_rows = out_0.rearrange("(p t) j -> p t j", t=4)
+        out_words = out_1[0].rearrange("p n t -> p (n t)").bitcast(I32)
+        for c0, w in G_CHUNKS:
+            half, off = divmod(c0, 256)
+            lcols = slice(c0 // 16, (c0 + w) // 16)
+            ga = sb("ga%d" % c0, [P, 4, w], F32)
+            gb = sb("gb%d" % c0, [P, 4, w], F32)
+            for t in range(4):
+                nc.vector.tensor_tensor(ga[:, t, :], h_neg[t][:].indirect(n3_t[:, lcols]), xn[half][:, t, off : off + w], ALU.subtract)
+            for t in range(4):
+                nc.vector.tensor_tensor(gb[:, t, :], h_pos[t][:].indirect(n4_t[:, lcols]), ga[:, t, :], ALU.subtract)
+            for u in range(w // OUT_W):
+                c = c0 // OUT_W + u
+                cols = slice(OUT_W * c, OUT_W * c + OUT_W)
+                sub = slice(OUT_W * u, OUT_W * u + OUT_W)
+                hsub = slice(off + OUT_W * u, off + OUT_W * u + OUT_W)
+                ga_c, gb_c, xc, yc = ga[:, :, sub], gb[:, :, sub], xn[half][:, :, hsub], yp[half][:, :, hsub]
+                sum_t = bank(4 + 2 * (c % 2))
+                add_transposed(sum_t, (yc, gb_c))
+                dif_t = bank(5 + 2 * (c % 2))
+                add_transposed(dif_t, (xc, ga_c, ga_c, gb_c))
+                q1 = ring.tile([P, 4, P], F32, name="q1")
+                q2 = ring.tile([P, 4, P], F32, name="q2")
+                nc.scalar.activation(q1[:].rearrange("p t j -> p (t j)"), sum_t[:], ACT.Square, scale=0.375)
+                nc.scalar.activation(q2[:].rearrange("p t j -> p (t j)"), dif_t[:], ACT.Square)
+                q = bank(c)
+                add_transposed(q, (q1[:], q2[:]))
+                r = ring.tile([P, 4 * OUT_W], F32, name="r")
+                nc.scalar.activation(r[:], q[:], ACT.Abs_reciprocal_sqrt, bias=quarter[:], scale=0.5)
+                ge = gb_c
+                res = ring.tile([P, 4, OUT_W], F32, name="res")
+                nc.vector.scalar_tensor_tensor(res[:], ge, -0.3125, r[:].rearrange("p (t j) -> p t j", t=4), ALU.mult, ALU.mult)
+                nc.sync.dma_start(out_rows[:, :, cols], res[:])
+                ob = ring.tile([P, OUT_W, 4], BF16, name="ob", align_bytes=64)
+                nc.scalar.copy(ob[:].rearrange("p (c i) t -> p c t i", i=4), res[:].rearrange("p t (c i) -> p c t i", i=4))
+                nc.vector.quantize_mx(out=out_codes[:, cols].bitcast(FP8X4), scales=out_scales[:, cols],
+                                      in_=ob[:].rearrange("p c t -> p (c t)"))
+                nc.sync.dma_start(out_words[:, cols], out_codes[:, cols].bitcast(I32))
+        for q in range(4):
+            eng = nc.sync if q % 2 == 0 else nc.scalar
+            eng.dma_start(out_2[0, 4 * q : 4 * q + 4, :].bitcast(I32), out_scales[32 * q : 32 * q + 4, :].bitcast(I32))

@@ -15,9 +15,11 @@ FP8X4 = mybir.dt.float8_e4m3fn_x4
 ALU = mybir.AluOpType
 ACT = mybir.ActivationFunctionType
 P = 128
-G_CHUNKS = ((0, 256), (256, 128), (384, 128))
+Z_CHUNKS = ((0, 256), (256, 128), (384, 128))
 OUT_W = 128
-G_BUFS = 4
+GA_BUFS = 2
+GB_BUFS = 3
+GW_BUFS = 2
 
 
 def tile_picked_twtcrossbstd_none_po_kernel(
@@ -26,7 +28,7 @@ def tile_picked_twtcrossbstd_none_po_kernel(
     nc = tc.nc
     with ExitStack() as ctx:
         keep = ctx.enter_context(tc.tile_pool(name="keep", bufs=1))
-        ring = ctx.enter_context(tc.tile_pool(name="ring", bufs=G_BUFS))
+        ring = ctx.enter_context(tc.tile_pool(name="ring", bufs=4))
         psum = ctx.enter_context(tc.psum_pool(name="psum", bufs=1))
 
         def sb(name, shape, dtype):
@@ -57,7 +59,7 @@ def tile_picked_twtcrossbstd_none_po_kernel(
             )
 
         xs = sb("xs", [P, T], U8)
-        nc.gpsimd.memset(xs[:].bitcast(I32), 0)
+        nc.vector.memset(xs[:].bitcast(I32), 0)
         quarter = sb("quarter", [P, 1], F32)
         nc.gpsimd.memset(quarter[:], 0.25)
         warm = sb("warm", [P, 1], F32)
@@ -75,9 +77,11 @@ def tile_picked_twtcrossbstd_none_po_kernel(
             w_raw[name, half] = raw
 
         offs_t = load_list("offs_t", offs)
-        load_weight_half("a", wa, 0)
+        w1w_raw = sb("w1w_raw", [P, N], U32)
+        nc.sync.dma_start(w1w_raw[:].bitcast(I32), w1_words[0].rearrange("p n t -> p (n t)").bitcast(I32))
         load_scale_rows(xs, x_scales)
         two_t = load_list("two_t", two)
+        load_weight_half("a", wa, 0)
         xw = sb("xw", [P, T], U32)
         nc.sync.dma_start(xw[:].bitcast(I32), x_words[0].rearrange("p n t -> p (n t)").bitcast(I32))
         load_weight_half("a", wa, 1)
@@ -87,15 +91,16 @@ def tile_picked_twtcrossbstd_none_po_kernel(
         nc.sync.dma_start(gt_t[:], gt.rearrange("(p t) o -> p (t o)", t=4))
         n1_t = load_list("n1_t", n1)
         n2_t = load_list("n2_t", n2)
-        w1w_raw = sb("w1w_raw", [P, N], U32)
-        nc.sync.dma_start(w1w_raw[:].bitcast(I32), w1_words[0].rearrange("p n t -> p (n t)").bitcast(I32))
         load_scale_rows(w1s_raw, w1_scales)
         n3_t = load_list("n3_t", n3)
         n4_t = load_list("n4_t", n4)
 
+        w1w = sb("w1w", [P, N], U32)
+        deal_words(w1w[:], w1w_raw[:])
         picked_w, picked_s = {}, {}
-        for name, lst in (("a", offs_t), ("b", two_t)):
-            g = sb("gs_" + name, [P, S], U8)
+
+        def pick_scales(name, lst, tag):
+            g = keep.tile([P, S], U8, name="gs_" + name, tag=tag, align_bytes=64)
             nc.vector.tensor_copy(g[:], xs[:].indirect(lst[:]))
             picked_s[name] = sb("ds_" + name, [P, S], U8)
             deal_scales(picked_s[name][:], g[:])
@@ -128,39 +133,50 @@ def tile_picked_twtcrossbstd_none_po_kernel(
                 out=dst, lhsT=picked_w[name][:, rows].bitcast(FP8X4), lhsT_scale=picked_s[name][:, rows],
                 rhs=w_codes[name][:, cols].bitcast(FP8X4), rhs_scale=w_scales[name][:, cols], start=True, stop=True)
 
+        pick_scales("a", offs_t, "gs_a")
+        pick_scales("b", two_t, "gs_b")
         quantise_weight_half("a", 0, False)
         pick_words("a", offs_t, "gw_a")
         quantise_weight_half("a", 1, False)
         pick_words("b", two_t, "wa_bf1")
         quantise_weight_half("b", 0, False)
+        quantise_weight_half("b", 1, True)
         y = [sb("y%d" % t, [P, H], F32) for t in range(4)]
         d = [sb("d%d" % t, [P, H], F32) for t in range(4)]
-        for t in range(4):
+
+        def make_y(t):
             acc = bank(t)
             first_product(acc[:], "a", t, slice(0, H))
             nc.scalar.activation(y[t][:], acc[:], ACT.Copy, scale=gt_t[:, t : t + 1])
-        quantise_weight_half("b", 1, True)
-        for half in range(2):
-            cols = slice(256 * half, 256 * half + 256)
-            for pair in range(2):
-                acc = bank(4 + 2 * half + pair)
-                for u in range(2):
-                    first_product(acc[:, 256 * u : 256 * u + 256], "b", 2 * pair + u, cols)
-                for u in range(2):
-                    nc.scalar.activation(d[2 * pair + u][:, cols], acc[:, 256 * u : 256 * u + 256], ACT.Copy, scale=0.75)
 
-        w1w = sb("w1w", [P, N], U32)
-        deal_words(w1w[:], w1w_raw[:])
+        def make_d(half, pair):
+            cols = slice(256 * half, 256 * half + 256)
+            acc = bank(4 + 2 * half + pair)
+            for u in range(2):
+                first_product(acc[:, 256 * u : 256 * u + 256], "b", 2 * pair + u, cols)
+            for u in range(2):
+                nc.scalar.activation(d[2 * pair + u][:, cols], acc[:, 256 * u : 256 * u + 256], ACT.Copy, scale=0.75)
+
+        for pair in range(2):
+            make_y(2 * pair)
+            make_y(2 * pair + 1)
+            make_d(0, pair)
+        for pair in range(2):
+            make_d(1, pair)
+
         w1s = sb("w1s", [P, N], U8)
         deal_scales(w1s[:], w1s_raw[:])
 
-        h_pos = [sb("hp%d" % t, [P, H], F32) for t in range(4)]
-        h_neg = [sb("hn%d" % t, [P, H], F32) for t in range(4)]
-        xn = [sb("xn%d" % c, [P, 4, 256], F32) for c in range(2)]
-        yp = [sb("yp%d" % c, [P, 4, 256], F32) for c in range(2)]
-        for half in range(2):
-            w = 256
-            c0 = w * half
+        def add_transposed(dst, term, first=False, last=False):
+            for u in range(2):
+                nc.tensor.matmul(dst[:, P * u : P * u + P], lhsT=term[:, u, :], rhs=ident[:],
+                                 start=(first and u == 0), stop=(last and u == 1), is_transpose=True)
+
+        sums = {}
+        h = [sb("h%d" % t, [P, H], F32) for t in range(4)]
+        xn = [sb("xn%d" % c, [P, 4, OUT_W], F32) for c in range(4)]
+        yp = [sb("yp%d" % c, [P, 4, OUT_W], F32) for c in range(4)]
+        for c0, w in Z_CHUNKS:
             cols = slice(c0, c0 + w)
             lcols = slice(c0 // 16, (c0 + w) // 16)
             g1 = sb("zg1_%d" % c0, [P, 4, w], F32)
@@ -177,70 +193,72 @@ def tile_picked_twtcrossbstd_none_po_kernel(
             zc = sb("zc%d" % c0, [P, w], U32)
             zs = sb("zs%d" % c0, [P, w], U8)
             nc.vector.quantize_mx(out=zc[:].bitcast(FP8X4), scales=zs[:], in_=zb[:].rearrange("p c t -> p (c t)"))
-            accs = [bank(2 * half + pair) for pair in range(2)]
-            parts = [accs[t // 2][:, w * (t % 2) : w * (t % 2) + w] for t in range(4)]
-            for t in range(4):
-                rows = slice(P * t, P * t + P)
-                nc.tensor.matmul_mx(
-                    out=parts[t], lhsT=w1w[:, rows].bitcast(FP8X4), lhsT_scale=w1s[:, rows],
-                    rhs=zc[:].bitcast(FP8X4), rhs_scale=zs[:], start=True, stop=True)
-            for t in range(4):
-                nc.scalar.activation(h_neg[t][:, cols], parts[t], ACT.Copy, scale=-1.0)
-            for t in range(4):
-                nc.scalar.copy(h_pos[t][:, cols], parts[t])
-            for pair in range(2):
-                nc.scalar.activation(xn[half][:, 2 * pair : 2 * pair + 2, :].rearrange("p t j -> p (t j)"), accs[pair][:],
-                                     ACT.Copy, scale=-11.0 / 5.0)
-            for pair in range(2):
-                nc.scalar.activation(yp[half][:, 2 * pair : 2 * pair + 2, :].rearrange("p t j -> p (t j)"), accs[pair][:],
-                                     ACT.Copy, scale=8.0 / 15.0)
-
-        def add_transposed(dst, terms):
-            for t in range(4):
-                for n, term in enumerate(terms):
-                    nc.tensor.matmul(dst[:, P * t : P * t + P], lhsT=term[:, t, :], rhs=ident[:],
-                                     start=(n == 0), stop=(n == len(terms) - 1), is_transpose=True)
+            chunks = range(c0 // OUT_W, (c0 + w) // OUT_W)
+            accs = {c: bank(c) for c in chunks}
+            for c in chunks:
+                sub = slice(OUT_W * c - c0, OUT_W * c - c0 + OUT_W)
+                for t in range(4):
+                    rows = slice(P * t, P * t + P)
+                    nc.tensor.matmul_mx(
+                        out=accs[c][:, rows], lhsT=w1w[:, rows].bitcast(FP8X4), lhsT_scale=w1s[:, rows],
+                        rhs=zc[:, sub].bitcast(FP8X4), rhs_scale=zs[:, sub], start=True, stop=True)
+            for c in chunks:
+                for t in range(4):
+                    nc.scalar.copy(h[t][:, OUT_W * c : OUT_W * c + OUT_W], accs[c][:, P * t : P * t + P])
+                nc.scalar.activation(xn[c][:].rearrange("p t j -> p (t j)"), accs[c][:], ACT.Copy, scale=-11.0 / 5.0)
+                nc.scalar.activation(yp[c][:].rearrange("p t j -> p (t j)"), accs[c][:], ACT.Copy, scale=8.0 / 15.0)
+            for c in chunks:
+                for pair in range(2):
+                    tiles = slice(2 * pair, 2 * pair + 2)
+                    acc = bank((4 + 2 * c + pair) % 8)
+                    add_transposed(acc[:, 0:256], yp[c][:, tiles, :], first=True)
+                    add_transposed(acc[:, 256:512], xn[c][:, tiles, :])
+                    sums[c, pair] = acc
 
         out_codes = sb("out_codes", [P, H], U32)
         out_scales = sb("out_scales", [P, H], U8)
         out_rows = out_0.rearrange("(p t) j -> p t j", t=4)
         out_words = out_1[0].rearrange("p n t -> p (n t)").bitcast(I32)
-        for c0, w in G_CHUNKS:
-            half, off = divmod(c0, 256)
-            lcols = slice(c0 // 16, (c0 + w) // 16)
-            ga = sb("ga%d" % c0, [P, 4, w], F32)
-            gb = sb("gb%d" % c0, [P, 4, w], F32)
-            for t in range(4):
-                nc.vector.tensor_tensor(ga[:, t, :], h_neg[t][:].indirect(n3_t[:, lcols]), xn[half][:, t, off : off + w], ALU.subtract)
-            for t in range(4):
-                nc.vector.tensor_tensor(gb[:, t, :], h_pos[t][:].indirect(n4_t[:, lcols]), ga[:, t, :], ALU.subtract)
-            for u in range(w // OUT_W):
-                c = c0 // OUT_W + u
-                cols = slice(OUT_W * c, OUT_W * c + OUT_W)
-                sub = slice(OUT_W * u, OUT_W * u + OUT_W)
-                hsub = slice(off + OUT_W * u, off + OUT_W * u + OUT_W)
-                ga_c, gb_c, xc, yc = ga[:, :, sub], gb[:, :, sub], xn[half][:, :, hsub], yp[half][:, :, hsub]
-                sum_t = bank(4 + 2 * (c % 2))
-                add_transposed(sum_t, (yc, gb_c))
-                dif_t = bank(5 + 2 * (c % 2))
-                add_transposed(dif_t, (xc, ga_c, ga_c, gb_c))
-                q1 = ring.tile([P, 4, P], F32, name="q1")
-                q2 = ring.tile([P, 4, P], F32, name="q2")
-                nc.scalar.activation(q1[:].rearrange("p t j -> p (t j)"), sum_t[:], ACT.Square, scale=0.375)
-                nc.scalar.activation(q2[:].rearrange("p t j -> p (t j)"), dif_t[:], ACT.Square)
-                q = bank(c)
-                add_transposed(q, (q1[:], q2[:]))
-                r = ring.tile([P, 4 * OUT_W], F32, name="r")
-                nc.scalar.activation(r[:], q[:], ACT.Abs_reciprocal_sqrt, bias=quarter[:], scale=0.5)
-                ge = gb_c
-                res = ring.tile([P, 4, OUT_W], F32, name="res")
-                nc.vector.scalar_tensor_tensor(res[:], ge, -0.3125, r[:].rearrange("p (t j) -> p t j", t=4), ALU.mult, ALU.mult)
-                nc.sync.dma_start(out_rows[:, :, cols], res[:])
-                ob = ring.tile([P, OUT_W, 4], BF16, name="ob", align_bytes=64)
-                nc.scalar.copy(ob[:].rearrange("p (c i) t -> p c t i", i=4), res[:].rearrange("p t (c i) -> p c t i", i=4))
-                nc.vector.quantize_mx(out=out_codes[:, cols].bitcast(FP8X4), scales=out_scales[:, cols],
-                                      in_=ob[:].rearrange("p c t -> p (c t)"))
-                nc.sync.dma_start(out_words[:, cols], out_codes[:, cols].bitcast(I32))
+        for c in range(H // OUT_W):
+            cols = slice(OUT_W * c, OUT_W * c + OUT_W)
+            lcols = slice(OUT_W * c // 16, OUT_W * (c + 1) // 16)
+            res = ring.tile([P, 4, OUT_W], F32, name="res")
+            for pair in range(2):
+                ga = ring.tile([P, 2, OUT_W], F32, name="ga", bufs=GA_BUFS)
+                gb = ring.tile([P, 2, OUT_W], F32, name="gb", bufs=GB_BUFS)
+                for u in range(2):
+                    t = 2 * pair + u
+                    nc.vector.tensor_tensor(ga[:, u, :], h[t][:].indirect(n3_t[:, lcols]), xn[c][:, t, :], ALU.add)
+                for u in range(2):
+                    t = 2 * pair + u
+                    nc.vector.tensor_tensor(gb[:, u, :], h[t][:].indirect(n4_t[:, lcols]), ga[:, u, :], ALU.add)
+                gw = ring.tile([P, 2, OUT_W], F32, name="gw", bufs=GW_BUFS)
+                nc.vector.scalar_tensor_tensor(gw[:], ga[:], -2.0, gb[:], ALU.mult, ALU.add)
+                acc = sums[c, pair]
+                add_transposed(acc[:, 0:256], gb)
+                add_transposed(acc[:, 256:512], gw, last=True)
+                q1 = ring.tile([P, 2, P], F32, name="q1")
+                q2 = ring.tile([P, 2, P], F32, name="q2")
+                nc.scalar.activation(q1[:].rearrange("p t j -> p (t j)"), acc[:, 0:256], ACT.Square, scale=0.375)
+                nc.scalar.activation(q2[:].rearrange("p t j -> p (t j)"), acc[:, 256:512], ACT.Square)
+                q = bank((4 + 2 * c + pair) % 8)
+                add_transposed(q[:, 0:256], q1, first=True)
+                add_transposed(q[:, 0:256], q2, last=True)
+                r = ring.tile([P, 2 * OUT_W], F32, name="r")
+                nc.scalar.activation(r[:], q[:, 0:256], ACT.Abs_reciprocal_sqrt, bias=quarter[:], scale=0.5)
+                nc.vector.scalar_tensor_tensor(res[:, 2 * pair : 2 * pair + 2, :].rearrange("p t j -> p (t j)"),
+                                               gb[:].rearrange("p t j -> p (t j)"), -0.3125, r[:], ALU.mult, ALU.mult)
+            nc.sync.dma_start(out_rows[:, :, cols], res[:])
+            ob = ring.tile([P, OUT_W, 4], BF16, name="ob", align_bytes=64)
+            dst = ob[:].rearrange("p (c i) t -> p c t i", i=4)
+            src = res[:].rearrange("p t (c i) -> p c t i", i=4)
+            if c == H // OUT_W - 1:
+                nc.vector.tensor_copy(dst, src)
+            else:
+                nc.scalar.copy(dst, src)
+            nc.vector.quantize_mx(out=out_codes[:, cols].bitcast(FP8X4), scales=out_scales[:, cols],
+                                  in_=ob[:].rearrange("p c t -> p (c t)"))
+            nc.sync.dma_start(out_words[:, cols], out_codes[:, cols].bitcast(I32))
         for q in range(4):
             eng = nc.sync if q % 2 == 0 else nc.scalar
             eng.dma_start(out_2[0, 4 * q : 4 * q + 4, :].bitcast(I32), out_scales[32 * q : 32 * q + 4, :].bitcast(I32))

@@ -15,11 +15,13 @@ FP8X4 = mybir.dt.float8_e4m3fn_x4
 ALU = mybir.AluOpType
 ACT = mybir.ActivationFunctionType
 P = 128
-Z_CHUNKS = ((0, 256), (256, 128), (384, 128))
+OPT = {'ev':("x0 y0","x1","y1","x2 y2 x3 y3"),'wide':(0,),'gb':6,'lag':(0,1,1),'ilv':(2,3),'gw':3,'ga':3,'order':'offs w1w xs two xw a0 b0 a1 b1 gt n1 n2 w1s n3 n4','holdb':'gwb'}
+Z_CHUNKS = OPT.get("z", ((0, 256), (256, 128), (384, 128)))
+KINDS = OPT.get("kinds", "VVVVVVVV")
 OUT_W = 128
-GA_BUFS = 2
-GB_BUFS = 3
-GW_BUFS = 2
+GA_BUFS = OPT.get("ga", 2)
+GB_BUFS = OPT.get("gb", 3)
+GW_BUFS = OPT.get("gw", 2)
 
 
 def tile_picked_twtcrossbstd_none_po_kernel(
@@ -76,24 +78,26 @@ def tile_picked_twtcrossbstd_none_po_kernel(
             nc.sync.dma_start(raw[:], src.rearrange("(p j) c -> p j c", j=4)[:, :, 256 * half : 256 * half + 256])
             w_raw[name, half] = raw
 
-        offs_t = load_list("offs_t", offs)
         w1w_raw = sb("w1w_raw", [P, N], U32)
-        nc.sync.dma_start(w1w_raw[:].bitcast(I32), w1_words[0].rearrange("p n t -> p (n t)").bitcast(I32))
-        load_scale_rows(xs, x_scales)
-        two_t = load_list("two_t", two)
-        load_weight_half("a", wa, 0)
         xw = sb("xw", [P, T], U32)
-        nc.sync.dma_start(xw[:].bitcast(I32), x_words[0].rearrange("p n t -> p (n t)").bitcast(I32))
-        load_weight_half("a", wa, 1)
-        load_weight_half("b", wb, 0)
-        load_weight_half("b", wb, 1)
         gt_t = sb("gt_t", [P, 4], F32)
-        nc.sync.dma_start(gt_t[:], gt.rearrange("(p t) o -> p (t o)", t=4))
-        n1_t = load_list("n1_t", n1)
-        n2_t = load_list("n2_t", n2)
-        load_scale_rows(w1s_raw, w1_scales)
-        n3_t = load_list("n3_t", n3)
-        n4_t = load_list("n4_t", n4)
+        lists = {}
+        for name in OPT.get("order", "offs w1w xs two a0 xw a1 b0 b1 gt n1 n2 w1s n3 n4").split():
+            if name == "w1w":
+                nc.sync.dma_start(w1w_raw[:].bitcast(I32), w1_words[0].rearrange("p n t -> p (n t)").bitcast(I32))
+            elif name == "xw":
+                nc.sync.dma_start(xw[:].bitcast(I32), x_words[0].rearrange("p n t -> p (n t)").bitcast(I32))
+            elif name == "xs":
+                load_scale_rows(xs, x_scales)
+            elif name == "w1s":
+                load_scale_rows(w1s_raw, w1_scales)
+            elif name == "gt":
+                nc.sync.dma_start(gt_t[:], gt.rearrange("(p t) o -> p (t o)", t=4))
+            elif name[0] in "ab":
+                load_weight_half(name[0], wa if name[0] == "a" else wb, int(name[1]))
+            else:
+                lists[name] = load_list(name + "_t", dict(offs=offs, two=two, n1=n1, n2=n2, n3=n3, n4=n4)[name])
+        offs_t, two_t, n1_t, n2_t, n3_t, n4_t = [lists[x] for x in "offs two n1 n2 n3 n4".split()]
 
         w1w = sb("w1w", [P, N], U32)
         deal_words(w1w[:], w1w_raw[:])
@@ -137,17 +141,20 @@ def tile_picked_twtcrossbstd_none_po_kernel(
         pick_scales("b", two_t, "gs_b")
         quantise_weight_half("a", 0, False)
         pick_words("a", offs_t, "gw_a")
-        quantise_weight_half("a", 1, False)
-        pick_words("b", two_t, "wa_bf1")
+        quantise_weight_half("a", 1, OPT.get("wa1v", False))
+        pick_words("b", two_t, OPT.get("holdb", "wa_bf1"))
         quantise_weight_half("b", 0, False)
-        quantise_weight_half("b", 1, True)
+        quantise_weight_half("b", 1, OPT.get("wb1v", True))
         y = [sb("y%d" % t, [P, H], F32) for t in range(4)]
         d = [sb("d%d" % t, [P, H], F32) for t in range(4)]
 
         def make_y(t):
             acc = bank(t)
             first_product(acc[:], "a", t, slice(0, H))
-            nc.scalar.activation(y[t][:], acc[:], ACT.Copy, scale=gt_t[:, t : t + 1])
+            if t in OPT.get("yv", ()):
+                nc.vector.tensor_scalar(y[t][:], acc[:], gt_t[:, t : t + 1], None, ALU.mult)
+            else:
+                nc.scalar.activation(y[t][:], acc[:], ACT.Copy, scale=gt_t[:, t : t + 1])
 
         def make_d(half, pair):
             cols = slice(256 * half, 256 * half + 256)
@@ -155,41 +162,81 @@ def tile_picked_twtcrossbstd_none_po_kernel(
             for u in range(2):
                 first_product(acc[:, 256 * u : 256 * u + 256], "b", 2 * pair + u, cols)
             for u in range(2):
-                nc.scalar.activation(d[2 * pair + u][:, cols], acc[:, 256 * u : 256 * u + 256], ACT.Copy, scale=0.75)
+                if (half, pair) in OPT.get("dv", ()):
+                    nc.vector.tensor_scalar(d[2 * pair + u][:, cols], acc[:, 256 * u : 256 * u + 256], 0.75, None, ALU.mult)
+                else:
+                    nc.scalar.activation(d[2 * pair + u][:, cols], acc[:, 256 * u : 256 * u + 256], ACT.Copy, scale=0.75)
 
-        for pair in range(2):
-            make_y(2 * pair)
-            make_y(2 * pair + 1)
-            make_d(0, pair)
-        for pair in range(2):
-            make_d(1, pair)
+        for name in OPT.get("eo", "y0 y1 d00 y2 y3 d01 d10 d11").split():
+            if name[0] == "y":
+                make_y(int(name[1]))
+            else:
+                make_d(int(name[1]), int(name[2]))
 
         w1s = sb("w1s", [P, N], U8)
         deal_scales(w1s[:], w1s_raw[:])
 
-        def add_transposed(dst, term, first=False, last=False):
-            for u in range(2):
-                nc.tensor.matmul(dst[:, P * u : P * u + P], lhsT=term[:, u, :], rhs=ident[:],
-                                 start=(first and u == 0), stop=(last and u == 1), is_transpose=True)
+        def add_transposed(dst, blocks, first=False, last=False):
+            for u, block in enumerate(blocks):
+                nc.tensor.matmul(dst[:, P * u : P * u + P], lhsT=block, rhs=ident[:],
+                                 start=(first and u == 0), stop=(last and u == len(blocks) - 1), is_transpose=True)
 
-        sums = {}
+        wide = OPT.get("wide", ())
+        holds = OPT.get("holds", {})
+
+        def held(name, shape, dtype):
+            return keep.tile(shape, dtype, name=name, tag=holds.get(name, name), align_bytes=64)
+
+        def unit_blocks(k):
+            half, j = divmod(k, 4)
+            if half in wide:
+                return [(j, 2 * half), (j, 2 * half + 1)]
+            return [(2 * (j % 2), k // 2), (2 * (j % 2) + 1, k // 2)]
+
+        sums, h_banks, made = {}, {}, set()
         h = [sb("h%d" % t, [P, H], F32) for t in range(4)]
-        xn = [sb("xn%d" % c, [P, 4, OUT_W], F32) for c in range(4)]
-        yp = [sb("yp%d" % c, [P, 4, OUT_W], F32) for c in range(4)]
+        xn = [sb("xn%d" % c, [P, 4, 256], F32) for c in range(2)]
+        yp = [sb("yp%d" % c, [P, 4, 256], F32) for c in range(2)]
+
+        def part(tiles, t, c):
+            return tiles[c // 2][:, t, P * (c % 2) : P * (c % 2) + P]
+
+        def h_terms(k):
+            acc = bank((4 + k) % 8)
+            add_transposed(acc[:, 0:256], [part(yp, t, c) for t, c in unit_blocks(k)], first=True)
+            add_transposed(acc[:, 256:512], [part(xn, t, c) for t, c in unit_blocks(k)])
+            sums[k] = acc
+
         for c0, w in Z_CHUNKS:
             cols = slice(c0, c0 + w)
             lcols = slice(c0 // 16, (c0 + w) // 16)
-            g1 = sb("zg1_%d" % c0, [P, 4, w], F32)
-            g2 = sb("zg2_%d" % c0, [P, 4, w], F32)
+            g1 = held("zg1_%d" % c0, [P, 4, w], F32)
+            g2 = held("zg2_%d" % c0, [P, 4, w], F32)
             for t in range(4):
                 nc.vector.tensor_tensor(g2[:, t, :], y[t][:].indirect(n1_t[:, lcols]), d[t][:, cols], ALU.mult)
             for t in range(4):
                 nc.vector.tensor_tensor(g1[:, t, :], d[t][:].indirect(n2_t[:, lcols]), y[t][:, cols], ALU.mult)
-            zb = sb("zb%d" % c0, [P, w, 4], BF16)
-            nc.vector.tensor_tensor(
-                zb[:].rearrange("p (c i) t -> p c t i", i=2),
-                g1[:].rearrange("p t (c i) -> p c t i", i=2),
-                g2[:].rearrange("p t (c i) -> p c t i", i=2), ALU.subtract)
+            zb = held("zb%d" % c0, [P, w, 4], BF16)
+            if c0 in OPT.get("pesub", ()):
+                g2n = sb("g2n%d" % c0, [P, 4, w], F32)
+                nc.scalar.activation(g2n[:], g2[:], ACT.Copy, scale=-1.0)
+                back = bank(6)
+                for u in range(w // P):
+                    zt = bank(4 + u)
+                    add_transposed(zt, [g2n[:, t, P * u : P * u + P] for t in range(4)], first=True)
+                    add_transposed(zt, [g1[:, t, P * u : P * u + P] for t in range(4)], last=True)
+                    ztb = sb("ztb%d_%d" % (c0, u), [P, 2, P, 2], BF16)
+                    nc.scalar.activation(ztb[:], zt[:].rearrange("j (u e p) -> j u p e", u=2, e=2), ACT.Copy)
+                    words = ztb[:].rearrange("j u p e -> j (u p e)").bitcast(F32)
+                    for v in range(2):
+                        nc.tensor.transpose(back[:, 256 * u + P * v : 256 * u + P * v + P], words[:, P * v : P * v + P], ident[:])
+                nc.scalar.copy(zb[:].rearrange("p c t -> p (c t)").bitcast(F32).rearrange("p (u j v) -> p u j v", v=2, j=P),
+                               back[:, 0 : 2 * w].rearrange("p (u v j) -> p u j v", v=2, j=P))
+            else:
+                nc.vector.tensor_tensor(
+                    zb[:].rearrange("p (c i) t -> p c t i", i=2),
+                    g1[:].rearrange("p t (c i) -> p c t i", i=2),
+                    g2[:].rearrange("p t (c i) -> p c t i", i=2), ALU.subtract)
             zc = sb("zc%d" % c0, [P, w], U32)
             zs = sb("zs%d" % c0, [P, w], U8)
             nc.vector.quantize_mx(out=zc[:].bitcast(FP8X4), scales=zs[:], in_=zb[:].rearrange("p c t -> p (c t)"))
@@ -205,60 +252,101 @@ def tile_picked_twtcrossbstd_none_po_kernel(
             for c in chunks:
                 for t in range(4):
                     nc.scalar.copy(h[t][:, OUT_W * c : OUT_W * c + OUT_W], accs[c][:, P * t : P * t + P])
-                nc.scalar.activation(xn[c][:].rearrange("p t j -> p (t j)"), accs[c][:], ACT.Copy, scale=-11.0 / 5.0)
-                nc.scalar.activation(yp[c][:].rearrange("p t j -> p (t j)"), accs[c][:], ACT.Copy, scale=8.0 / 15.0)
-            for c in chunks:
-                for pair in range(2):
-                    tiles = slice(2 * pair, 2 * pair + 2)
-                    acc = bank((4 + 2 * c + pair) % 8)
-                    add_transposed(acc[:, 0:256], yp[c][:, tiles, :], first=True)
-                    add_transposed(acc[:, 256:512], xn[c][:, tiles, :])
-                    sums[c, pair] = acc
+                h_banks[c] = accs[c]
+                for name in OPT.get("ev", ("x0 y0", "x1 y1", "x2 y2", "x3 y3"))[c].split():
+                    cc = int(name[1])
+                    view = h_banks[cc][:].rearrange("p (t j) -> p t j", t=4)
+                    dst = (xn if name[0] == "x" else yp)[cc // 2][:, :, P * (cc % 2) : P * (cc % 2) + P]
+                    nc.scalar.activation(dst, view, ACT.Copy, scale=-11.0 / 5.0 if name[0] == "x" else 8.0 / 15.0)
+                    made.add(name)
+            for k in range(8):
+                if k not in sums and all(s + str(c) in made for t, c in unit_blocks(k) for s in "xy"):
+                    h_terms(k)
 
         out_codes = sb("out_codes", [P, H], U32)
         out_scales = sb("out_scales", [P, H], U8)
         out_rows = out_0.rearrange("(p t) j -> p t j", t=4)
         out_words = out_1[0].rearrange("p n t -> p (n t)").bitcast(I32)
-        for c in range(H // OUT_W):
-            cols = slice(OUT_W * c, OUT_W * c + OUT_W)
-            lcols = slice(OUT_W * c // 16, OUT_W * (c + 1) // 16)
-            res = ring.tile([P, 4, OUT_W], F32, name="res")
-            for pair in range(2):
-                ga = ring.tile([P, 2, OUT_W], F32, name="ga", bufs=GA_BUFS)
-                gb = ring.tile([P, 2, OUT_W], F32, name="gb", bufs=GB_BUFS)
-                for u in range(2):
-                    t = 2 * pair + u
-                    nc.vector.tensor_tensor(ga[:, u, :], h[t][:].indirect(n3_t[:, lcols]), xn[c][:, t, :], ALU.add)
-                for u in range(2):
-                    t = 2 * pair + u
-                    nc.vector.tensor_tensor(gb[:, u, :], h[t][:].indirect(n4_t[:, lcols]), ga[:, u, :], ALU.add)
-                gw = ring.tile([P, 2, OUT_W], F32, name="gw", bufs=GW_BUFS)
+        res = [sb("res%d" % c, [P, 4, 256], F32) for c in range(2)]
+        gbs, qs = {}, {}
+
+        def stage_a(k):
+            blocks = unit_blocks(k)
+            acc = sums[k]
+            ga = ring.tile([P, 256], F32, name="ga", bufs=GA_BUFS)
+            gb = ring.tile([P, 256], F32, name="gb", bufs=GB_BUFS)
+            if k // 4 in wide:
+                t, c = blocks[0]
+                pieces = [(slice(0, 256), t, slice(8 * c, 8 * c + 16), xn[c // 2][:, t, :])]
+            else:
+                pieces = [(slice(P * u, P * u + P), t, slice(8 * c, 8 * c + 8), part(xn, t, c)) for u, (t, c) in enumerate(blocks)]
+            for dst, t, lcols, x in pieces:
+                nc.vector.tensor_tensor(ga[:, dst], h[t][:].indirect(n3_t[:, lcols]), x, ALU.add)
+            for dst, t, lcols, x in pieces:
+                nc.vector.tensor_tensor(gb[:, dst], h[t][:].indirect(n4_t[:, lcols]), ga[:, dst], ALU.add)
+            gw = ring.tile([P, 256], F32, name="gw", bufs=GW_BUFS)
+            two_of = lambda a: [a[:, 0:P], a[:, P : 2 * P]]
+            if KINDS[k] == "S":
+                nc.scalar.activation(gw[:], ga[:], ACT.Copy, scale=-2.0)
+                add_transposed(acc[:, 256:512], two_of(gw))
+                add_transposed(acc[:, 0:256], two_of(gb))
+                add_transposed(acc[:, 256:512], two_of(gb), last=True)
+            else:
                 nc.vector.scalar_tensor_tensor(gw[:], ga[:], -2.0, gb[:], ALU.mult, ALU.add)
-                acc = sums[c, pair]
-                add_transposed(acc[:, 0:256], gb)
-                add_transposed(acc[:, 256:512], gw, last=True)
-                q1 = ring.tile([P, 2, P], F32, name="q1")
-                q2 = ring.tile([P, 2, P], F32, name="q2")
-                nc.scalar.activation(q1[:].rearrange("p t j -> p (t j)"), acc[:, 0:256], ACT.Square, scale=0.375)
-                nc.scalar.activation(q2[:].rearrange("p t j -> p (t j)"), acc[:, 256:512], ACT.Square)
-                q = bank((4 + 2 * c + pair) % 8)
-                add_transposed(q[:, 0:256], q1, first=True)
-                add_transposed(q[:, 0:256], q2, last=True)
-                r = ring.tile([P, 2 * OUT_W], F32, name="r")
-                nc.scalar.activation(r[:], q[:, 0:256], ACT.Abs_reciprocal_sqrt, bias=quarter[:], scale=0.5)
-                nc.vector.scalar_tensor_tensor(res[:, 2 * pair : 2 * pair + 2, :].rearrange("p t j -> p (t j)"),
-                                               gb[:].rearrange("p t j -> p (t j)"), -0.3125, r[:], ALU.mult, ALU.mult)
-            nc.sync.dma_start(out_rows[:, :, cols], res[:])
-            ob = ring.tile([P, OUT_W, 4], BF16, name="ob", align_bytes=64)
+                add_transposed(acc[:, 0:256], two_of(gb))
+                add_transposed(acc[:, 256:512], two_of(gw), last=True)
+            gbs[k] = gb
+
+        def stage_b(k):
+            acc = sums[k]
+            q1 = ring.tile([P, 256], F32, name="q1")
+            q2 = ring.tile([P, 256], F32, name="q2")
+            nc.scalar.activation(q1[:], acc[:, 0:256], ACT.Square, scale=0.375)
+            nc.scalar.activation(q2[:], acc[:, 256:512], ACT.Square)
+            q = bank((4 + k) % 8)
+            add_transposed(q[:, 0:256], [q1[:, 0:P], q1[:, P : 2 * P]], first=True)
+            add_transposed(q[:, 0:256], [q2[:, 0:P], q2[:, P : 2 * P]], last=True)
+            qs[k] = q
+
+        def stage_c(k):
+            r = ring.tile([P, 256], F32, name="r")
+            nc.scalar.activation(r[:], qs[k][:, 0:256], ACT.Abs_reciprocal_sqrt, bias=quarter[:], scale=0.5)
+            (t0, c0), (t1, c1) = unit_blocks(k)
+            if k // 4 in wide:
+                nc.vector.scalar_tensor_tensor(res[k // 4][:, t0, :], gbs[k][:], -0.3125, r[:], ALU.mult, ALU.mult)
+            else:
+                off = P * (c0 % 2)
+                nc.vector.scalar_tensor_tensor(res[k // 4][:, t0 : t0 + 2, off : off + P], gbs[k][:].rearrange("p (u j) -> p u j", u=2),
+                                               -0.3125, r[:].rearrange("p (u j) -> p u j", u=2), ALU.mult, ALU.mult)
+
+        def stage_d(k):
+            if k // 4 in wide:
+                if k % 4 != 3:
+                    return
+                c0, w = 256 * (k // 4), 256
+            else:
+                if k % 2 != 1:
+                    return
+                c0, w = P * (k // 2), P
+            cols = slice(c0, c0 + w)
+            src = res[k // 4][:, :, c0 % 256 : c0 % 256 + w]
+            nc.sync.dma_start(out_rows[:, :, cols], src)
+            ob = sb("ob%d" % c0, [P, w, 4], BF16)
             dst = ob[:].rearrange("p (c i) t -> p c t i", i=4)
-            src = res[:].rearrange("p t (c i) -> p c t i", i=4)
-            if c == H // OUT_W - 1:
+            src = src.rearrange("p t (c i) -> p c t i", i=4)
+            if k // 2 in OPT.get("ilv", (3,)):
                 nc.vector.tensor_copy(dst, src)
             else:
                 nc.scalar.copy(dst, src)
             nc.vector.quantize_mx(out=out_codes[:, cols].bitcast(FP8X4), scales=out_scales[:, cols],
                                   in_=ob[:].rearrange("p c t -> p (c t)"))
             nc.sync.dma_start(out_words[:, cols], out_codes[:, cols].bitcast(I32))
+
+        lag = OPT.get("lag", (0, 0, 0))
+        for step in range(8 + max(lag)):
+            for stage, l in ((stage_a, 0), (stage_b, lag[0]), (stage_c, lag[1]), (stage_d, lag[2])):
+                if 0 <= step - l < 8:
+                    stage(step - l)
         for q in range(4):
             eng = nc.sync if q % 2 == 0 else nc.scalar
             eng.dma_start(out_2[0, 4 * q : 4 * q + 4, :].bitcast(I32), out_scales[32 * q : 32 * q + 4, :].bitcast(I32))

from contextlib import ExitStack

import concourse.mybir as mybir
from concourse.masks import make_identity

K, T, S, N, H = 512, 2048, 512, 512, 512
FLOPS = 2 * 3 * 512 * 512 * 512
F32 = mybir.dt.float32
BF16 = mybir.dt.bfloat16
I32 = mybir.dt.int32
U32 = mybir.dt.uint32
U16 = mybir.dt.uint16
U8 = mybir.dt.uint8
FP8X4 = mybir.dt.float8_e4m3fn_x4
ALU = mybir.AluOpType
ACT = mybir.ActivationFunctionType
P = 128
OPT = {'ev':("x0 y0","x1","y1","x2 y2 x3 y3"),'wide':(0,),'gb':6,'lag':(0,1,1),'ilv':(2,3),'gw':3,'ga':3,'order':'offs w1w xs two xw a0 b0 a1 b1 gt n1 n2 w1s n3 n4','holdb':'gwb'}
Z_CHUNKS = OPT.get("z", ((0, 256), (256, 128), (384, 128)))
KINDS = OPT.get("kinds", "VVVVVVVV")
OUT_W = 128
GA_BUFS = OPT.get("ga", 2)
GB_BUFS = OPT.get("gb", 3)
GW_BUFS = OPT.get("gw", 2)


def tile_picked_twtcrossbstd_none_po_kernel(
    tc, x_words, x_scales, wa, wb, gt, w1_words, w1_scales, offs, two, n1, n2, n3, n4, out_0, out_1, out_2
):
    nc = tc.nc
    with ExitStack() as ctx:
        keep = ctx.enter_context(tc.tile_pool(name="keep", bufs=1))
        ring = ctx.enter_context(tc.tile_pool(name="ring", bufs=4))
        psum = ctx.enter_context(tc.psum_pool(name="psum", bufs=1))

        def sb(name, shape, dtype):
            return keep.tile(shape, dtype, name=name, align_bytes=64)

        def bank(b):
            return psum.tile([P, 512], F32, name="bank%d" % b, tag="bank%d" % b)

        def load_list(name, src):
            tile = keep.tile([P, 32], U16, name=name)
            nc.sync.dma_start(tile[:], src)
            return tile

        def load_scale_rows(tile, src):
            for q in range(4):
                nc.sync.dma_start(tile[32 * q : 32 * q + 4, :].bitcast(I32), src[0, 4 * q : 4 * q + 4, :].bitcast(I32))

        def deal_words(dst, src):
            nc.vector.tensor_copy(
                dst.bitcast(I32).rearrange("p (t c i) -> p c t i", t=4, i=4),
                src.bitcast(I32).rearrange("p (c i t) -> p c t i", t=4, i=4),
            )

        def deal_scales(dst, src):
            nc.vector.tensor_copy(
                dst.rearrange("p (t c i) -> p c t i", t=4, i=16),
                src.rearrange("p (c i t) -> p c t i", t=4, i=16),
            )

        xs = sb("xs", [P, T], U8)
        nc.vector.memset(xs[:].bitcast(I32), 0)
        quarter = sb("quarter", [P, 1], F32)
        nc.gpsimd.memset(quarter[:], 0.25)
        warm = sb("warm", [P, 1], F32)
        nc.scalar.activation(warm[:], quarter[:], ACT.Abs_reciprocal_sqrt, bias=quarter[:], scale=0.5)
        w1s_raw = sb("w1s_raw", [P, N], U8)
        nc.vector.memset(w1s_raw[:].bitcast(I32), 0)
        ident = sb("ident", [P, P], F32)
        make_identity(nc, ident[:])

        w_raw = {}

        def load_weight_half(name, src, half):
            raw = sb("w%s_raw%d" % (name, half), [P, 4, 256], F32)
            nc.sync.dma_start(raw[:], src.rearrange("(p j) c -> p j c", j=4)[:, :, 256 * half : 256 * half + 256])
            w_raw[name, half] = raw

        w1w_raw = sb("w1w_raw", [P, N], U32)
        xw = sb("xw", [P, T], U32)
        gt_t = sb("gt_t", [P, 4], F32)
        lists = {}
        for name in OPT.get("order", "offs w1w xs two a0 xw a1 b0 b1 gt n1 n2 w1s n3 n4").split():
            if name == "w1w":
                nc.sync.dma_start(w1w_raw[:].bitcast(I32), w1_words[0].rearrange("p n t -> p (n t)").bitcast(I32))
            elif name == "xw":
                nc.sync.dma_start(xw[:].bitcast(I32), x_words[0].rearrange("p n t -> p (n t)").bitcast(I32))
            elif name == "xs":
                load_scale_rows(xs, x_scales)
            elif name == "w1s":
                load_scale_rows(w1s_raw, w1_scales)
            elif name == "gt":
                nc.sync.dma_start(gt_t[:], gt.rearrange("(p t) o -> p (t o)", t=4))
            elif name[0] in "ab":
                load_weight_half(name[0], wa if name[0] == "a" else wb, int(name[1]))
            else:
                lists[name] = load_list(name + "_t", dict(offs=offs, two=two, n1=n1, n2=n2, n3=n3, n4=n4)[name])
        offs_t, two_t, n1_t, n2_t, n3_t, n4_t = [lists[x] for x in "offs two n1 n2 n3 n4".split()]

        w1w = sb("w1w", [P, N], U32)
        deal_words(w1w[:], w1w_raw[:])
        picked_w, picked_s = {}, {}

        def pick_scales(name, lst, tag):
            g = keep.tile([P, S], U8, name="gs_" + name, tag=tag, align_bytes=64)
            nc.vector.tensor_copy(g[:], xs[:].indirect(lst[:]))
            picked_s[name] = sb("ds_" + name, [P, S], U8)
            deal_scales(picked_s[name][:], g[:])

        def pick_words(name, lst, tag):
            g = keep.tile([P, S], U32, name="gw_" + name, tag=tag, align_bytes=64)
            nc.vector.tensor_copy(g[:], xw[:].indirect(lst[:]))
            picked_w[name] = sb("dw_" + name, [P, S], U32)
            deal_words(picked_w[name][:], g[:])

        w_codes = {name: sb("wc_" + name, [P, H], U32) for name in "ab"}
        w_scales = {name: sb("ws_" + name, [P, H], U8) for name in "ab"}

        def quantise_weight_half(name, half, on_vector):
            grouped = keep.tile([P, 256, 4], BF16, name="w_bf", tag="w%s_bf%d" % (name, half), align_bytes=64)
            dst = grouped[:].rearrange("p (c i) j -> p c j i", i=4)
            src = w_raw[name, half][:].rearrange("p j (c i) -> p c j i", i=4)
            if on_vector:
                nc.vector.tensor_copy(dst, src)
            else:
                nc.scalar.copy(dst, src)
            cols = slice(256 * half, 256 * half + 256)
            nc.vector.quantize_mx(
                out=w_codes[name][:, cols].bitcast(FP8X4), scales=w_scales[name][:, cols],
                in_=grouped[:].rearrange("p c j -> p (c j)"))

        def first_product(dst, name, t, cols):
            rows = slice(P * t, P * t + P)
            nc.tensor.matmul_mx(
                out=dst, lhsT=picked_w[name][:, rows].bitcast(FP8X4), lhsT_scale=picked_s[name][:, rows],
                rhs=w_codes[name][:, cols].bitcast(FP8X4), rhs_scale=w_scales[name][:, cols], start=True, stop=True)

        pick_scales("a", offs_t, "gs_a")
        pick_scales("b", two_t, "gs_b")
        quantise_weight_half("a", 0, False)
        pick_words("a", offs_t, "gw_a")
        quantise_weight_half("a", 1, OPT.get("wa1v", False))
        pick_words("b", two_t, OPT.get("holdb", "wa_bf1"))
        quantise_weight_half("b", 0, False)
        quantise_weight_half("b", 1, OPT.get("wb1v", True))
        y = [sb("y%d" % t, [P, H], F32) for t in range(4)]
        d = [sb("d%d" % t, [P, H], F32) for t in range(4)]

        def make_y(t):
            acc = bank(t)
            first_product(acc[:], "a", t, slice(0, H))
            if t in OPT.get("yv", ()):
                nc.vector.tensor_scalar(y[t][:], acc[:], gt_t[:, t : t + 1], None, ALU.mult)
            else:
                nc.scalar.activation(y[t][:], acc[:], ACT.Copy, scale=gt_t[:, t : t + 1])

        def make_d(half, pair):
            cols = slice(256 * half, 256 * half + 256)
            acc = bank(4 + 2 * half + pair)
            for u in range(2):
                first_product(acc[:, 256 * u : 256 * u + 256], "b", 2 * pair + u, cols)
            for u in range(2):
                if (half, pair) in OPT.get("dv", ()):
                    nc.vector.tensor_scalar(d[2 * pair + u][:, cols], acc[:, 256 * u : 256 * u + 256], 0.75, None, ALU.mult)
                else:
                    nc.scalar.activation(d[2 * pair + u][:, cols], acc[:, 256 * u : 256 * u + 256], ACT.Copy, scale=0.75)

        for name in OPT.get("eo", "y0 y1 d00 y2 y3 d01 d10 d11").split():
            if name[0] == "y":
                make_y(int(name[1]))
            else:
                make_d(int(name[1]), int(name[2]))

        w1s = sb("w1s", [P, N], U8)
        deal_scales(w1s[:], w1s_raw[:])

        def add_transposed(dst, blocks, first=False, last=False):
            for u, block in enumerate(blocks):
                nc.tensor.matmul(dst[:, P * u : P * u + P], lhsT=block, rhs=ident[:],
                                 start=(first and u == 0), stop=(last and u == len(blocks) - 1), is_transpose=True)

        wide = OPT.get("wide", ())
        holds = OPT.get("holds", {})

        def held(name, shape, dtype):
            return keep.tile(shape, dtype, name=name, tag=holds.get(name, name), align_bytes=64)

        def unit_blocks(k):
            half, j = divmod(k, 4)
            if half in wide:
                return [(j, 2 * half), (j, 2 * half + 1)]
            return [(2 * (j % 2), k // 2), (2 * (j % 2) + 1, k // 2)]

        sums, h_banks, made = {}, {}, set()
        h = [sb("h%d" % t, [P, H], F32) for t in range(4)]
        xn = [sb("xn%d" % c, [P, 4, 256], F32) for c in range(2)]
        yp = [sb("yp%d" % c, [P, 4, 256], F32) for c in range(2)]

        def part(tiles, t, c):
            return tiles[c // 2][:, t, P * (c % 2) : P * (c % 2) + P]

        def h_terms(k):
            acc = bank((4 + k) % 8)
            add_transposed(acc[:, 0:256], [part(yp, t, c) for t, c in unit_blocks(k)], first=True)
            add_transposed(acc[:, 256:512], [part(xn, t, c) for t, c in unit_blocks(k)])
            sums[k] = acc

        for c0, w in Z_CHUNKS:
            cols = slice(c0, c0 + w)
            lcols = slice(c0 // 16, (c0 + w) // 16)
            g1 = held("zg1_%d" % c0, [P, 4, w], F32)
            g2 = held("zg2_%d" % c0, [P, 4, w], F32)
            for t in range(4):
                nc.vector.tensor_tensor(g2[:, t, :], y[t][:].indirect(n1_t[:, lcols]), d[t][:, cols], ALU.mult)
            for t in range(4):
                nc.vector.tensor_tensor(g1[:, t, :], d[t][:].indirect(n2_t[:, lcols]), y[t][:, cols], ALU.mult)
            zb = held("zb%d" % c0, [P, w, 4], BF16)
            if c0 in OPT.get("pesub", ()):
                g2n = sb("g2n%d" % c0, [P, 4, w], F32)
                nc.scalar.activation(g2n[:], g2[:], ACT.Copy, scale=-1.0)
                back = bank(6)
                for u in range(w // P):
                    zt = bank(4 + u)
                    add_transposed(zt, [g2n[:, t, P * u : P * u + P] for t in range(4)], first=True)
                    add_transposed(zt, [g1[:, t, P * u : P * u + P] for t in range(4)], last=True)
                    ztb = sb("ztb%d_%d" % (c0, u), [P, 2, P, 2], BF16)
                    nc.scalar.activation(ztb[:], zt[:].rearrange("j (u e p) -> j u p e", u=2, e=2), ACT.Copy)
                    words = ztb[:].rearrange("j u p e -> j (u p e)").bitcast(F32)
                    for v in range(2):
                        nc.tensor.transpose(back[:, 256 * u + P * v : 256 * u + P * v + P], words[:, P * v : P * v + P], ident[:])
                nc.scalar.copy(zb[:].rearrange("p c t -> p (c t)").bitcast(F32).rearrange("p (u j v) -> p u j v", v=2, j=P),
                               back[:, 0 : 2 * w].rearrange("p (u v j) -> p u j v", v=2, j=P))
            else:
                nc.vector.tensor_tensor(
                    zb[:].rearrange("p (c i) t -> p c t i", i=2),
                    g1[:].rearrange("p t (c i) -> p c t i", i=2),
                    g2[:].rearrange("p t (c i) -> p c t i", i=2), ALU.subtract)
            zc = sb("zc%d" % c0, [P, w], U32)
            zs = sb("zs%d" % c0, [P, w], U8)
            nc.vector.quantize_mx(out=zc[:].bitcast(FP8X4), scales=zs[:], in_=zb[:].rearrange("p c t -> p (c t)"))
            chunks = range(c0 // OUT_W, (c0 + w) // OUT_W)
            accs = {c: bank(c) for c in chunks}
            for c in chunks:
                sub = slice(OUT_W * c - c0, OUT_W * c - c0 + OUT_W)
                for t in range(4):
                    rows = slice(P * t, P * t + P)
                    nc.tensor.matmul_mx(
                        out=accs[c][:, rows], lhsT=w1w[:, rows].bitcast(FP8X4), lhsT_scale=w1s[:, rows],
                        rhs=zc[:, sub].bitcast(FP8X4), rhs_scale=zs[:, sub], start=True, stop=True)
            for c in chunks:
                for t in range(4):
                    nc.scalar.copy(h[t][:, OUT_W * c : OUT_W * c + OUT_W], accs[c][:, P * t : P * t + P])
                h_banks[c] = accs[c]
                for name in OPT.get("ev", ("x0 y0", "x1 y1", "x2 y2", "x3 y3"))[c].split():
                    cc = int(name[1])
                    view = h_banks[cc][:].rearrange("p (t j) -> p t j", t=4)
                    dst = (xn if name[0] == "x" else yp)[cc // 2][:, :, P * (cc % 2) : P * (cc % 2) + P]
                    nc.scalar.activation(dst, view, ACT.Copy, scale=-11.0 / 5.0 if name[0] == "x" else 8.0 / 15.0)
                    made.add(name)
            for k in range(8):
                if k not in sums and all(s + str(c) in made for t, c in unit_blocks(k) for s in "xy"):
                    h_terms(k)

        out_codes = sb("out_codes", [P, H], U32)
        out_scales = sb("out_scales", [P, H], U8)
        out_rows = out_0.rearrange("(p t) j -> p t j", t=4)
        out_words = out_1[0].rearrange("p n t -> p (n t)").bitcast(I32)
        res = [sb("res%d" % c, [P, 4, 256], F32) for c in range(2)]
        gbs, qs = {}, {}

        def stage_a(k):
            blocks = unit_blocks(k)
            acc = sums[k]
            ga = ring.tile([P, 256], F32, name="ga", bufs=GA_BUFS)
            gb = ring.tile([P, 256], F32, name="gb", bufs=GB_BUFS)
            if k // 4 in wide:
                t, c = blocks[0]
                pieces = [(slice(0, 256), t, slice(8 * c, 8 * c + 16), xn[c // 2][:, t, :])]
            else:
                pieces = [(slice(P * u, P * u + P), t, slice(8 * c, 8 * c + 8), part(xn, t, c)) for u, (t, c) in enumerate(blocks)]
            for dst, t, lcols, x in pieces:
                nc.vector.tensor_tensor(ga[:, dst], h[t][:].indirect(n3_t[:, lcols]), x, ALU.add)
            for dst, t, lcols, x in pieces:
                nc.vector.tensor_tensor(gb[:, dst], h[t][:].indirect(n4_t[:, lcols]), ga[:, dst], ALU.add)
            gw = ring.tile([P, 256], F32, name="gw", bufs=GW_BUFS)
            two_of = lambda a: [a[:, 0:P], a[:, P : 2 * P]]
            if KINDS[k] == "S":
                nc.scalar.activation(gw[:], ga[:], ACT.Copy, scale=-2.0)
                add_transposed(acc[:, 256:512], two_of(gw))
                add_transposed(acc[:, 0:256], two_of(gb))
                add_transposed(acc[:, 256:512], two_of(gb), last=True)
            else:
                nc.vector.scalar_tensor_tensor(gw[:], ga[:], -2.0, gb[:], ALU.mult, ALU.add)
                add_transposed(acc[:, 0:256], two_of(gb))
                add_transposed(acc[:, 256:512], two_of(gw), last=True)
            gbs[k] = gb

        def stage_b(k):
            acc = sums[k]
            q1 = ring.tile([P, 256], F32, name="q1")
            q2 = ring.tile([P, 256], F32, name="q2")
            nc.scalar.activation(q1[:], acc[:, 0:256], ACT.Square, scale=0.375)
            nc.scalar.activation(q2[:], acc[:, 256:512], ACT.Square)
            q = bank((4 + k) % 8)
            add_transposed(q[:, 0:256], [q1[:, 0:P], q1[:, P : 2 * P]], first=True)
            add_transposed(q[:, 0:256], [q2[:, 0:P], q2[:, P : 2 * P]], last=True)
            qs[k] = q

        def stage_c(k):
            r = ring.tile([P, 256], F32, name="r")
            nc.scalar.activation(r[:], qs[k][:, 0:256], ACT.Abs_reciprocal_sqrt, bias=quarter[:], scale=0.5)
            (t0, c0), (t1, c1) = unit_blocks(k)
            if k // 4 in wide:
                nc.vector.scalar_tensor_tensor(res[k // 4][:, t0, :], gbs[k][:], -0.3125, r[:], ALU.mult, ALU.mult)
            else:
                off = P * (c0 % 2)
                nc.vector.scalar_tensor_tensor(res[k // 4][:, t0 : t0 + 2, off : off + P], gbs[k][:].rearrange("p (u j) -> p u j", u=2),
                                               -0.3125, r[:].rearrange("p (u j) -> p u j", u=2), ALU.mult, ALU.mult)

        def stage_d(k):
            if k // 4 in wide:
                if k % 4 != 3:
                    return
                c0, w = 256 * (k // 4), 256
            else:
                if k % 2 != 1:
                    return
                c0, w = P * (k // 2), P
            cols = slice(c0, c0 + w)
            src = res[k // 4][:, :, c0 % 256 : c0 % 256 + w]
            nc.sync.dma_start(out_rows[:, :, cols], src)
            ob = sb("ob%d" % c0, [P, w, 4], BF16)
            dst = ob[:].rearrange("p (c i) t -> p c t i", i=4)
            src = src.rearrange("p t (c i) -> p c t i", i=4)
            if k // 2 in OPT.get("ilv", (3,)):
                nc.vector.tensor_copy(dst, src)
            else:
                nc.scalar.copy(dst, src)
            nc.vector.quantize_mx(out=out_codes[:, cols].bitcast(FP8X4), scales=out_scales[:, cols],
                                  in_=ob[:].rearrange("p c t -> p (c t)"))
            nc.sync.dma_start(out_words[:, cols], out_codes[:, cols].bitcast(I32))

        lag = OPT.get("lag", (0, 0, 0))
        for step in range(8 + max(lag)):
            for stage, l in ((stage_a, 0), (stage_b, lag[0]), (stage_c, lag[1]), (stage_d, lag[2])):
                if 0 <= step - l < 8:
                    stage(step - l)
        for q in range(4):
            eng = nc.sync if q % 2 == 0 else nc.scalar
            eng.dma_start(out_2[0, 4 * q : 4 * q + 4, :].bitcast(I32), out_scales[32 * q : 32 * q + 4, :].bitcast(I32))
